import numpy as np
import ml_dtypes

BF16 = ml_dtypes.bfloat16


def bf(x):
    return np.asarray(x, np.float32).astype(BF16)


def f32(x):
    return np.asarray(x, np.float32)


def f64(x):
    return np.asarray(x).astype(np.float64)


def striped(idx):
    return np.concatenate([l.reshape(-1, 16).T for l in idx])


def rows(idx, k):
    return np.tile(np.repeat(idx, 16, axis=0), (k // (16 * 8), 1))


def look(tab, idx):
    return np.take_along_axis(f64(tab), rows(idx, len(tab)), axis=1)


K, S, V, N, M = 256, 2048, 2048, 2048, 256


def setup_inputs():
    return {"tab": f32(np.random.standard_normal((K, S))), "w": bf(np.random.standard_normal((K, M)) / np.sqrt(K)), "b": f32(0.5 * np.random.standard_normal((M, 1))), "offs": striped(np.random.randint(0, S, (8, N)))}


def reference(tab, w, b, offs):
    idx = np.stack([g.T.reshape(-1) for g in np.split(offs, 8)])
    t = look(tab, idx)
    x = (t - 0.125) * 1.5
    y = f64(w).T @ x
    return y + f64(b)

@@ -1,0 +1,69 @@
+import concourse.mybir as mybir
+
+F32, BF16, U16 = mybir.dt.float32, mybir.dt.bfloat16, mybir.dt.uint16
+ADD, MULT = mybir.AluOpType.add, mybir.AluOpType.mult
+IDENTITY = mybir.ActivationFunctionType.Identity
+
+P = 128
+K, S, N, M = 256, 2048, 2048, 256
+ROW_BLOCKS = K // P
+OUT_BLOCKS = M // P
+PIECE = 512
+PIECES = N // PIECE
+PIECE_COLS = PIECE // 16
+PAIR = 2
+
+SHIFT, SCALE = 0.125, 1.5
+
+FLOPS = 2 * K * M * N + 2 * K * N + M * N
+
+
+def tile_lookup_deq_nrm_bias_kernel(tc, tab, w, b, offs, out):
+    nc = tc.nc
+    with (
+        tc.tile_pool(name="held", bufs=1) as held,
+        tc.tile_pool(name="looked_up", bufs=2 * PAIR) as looked_up,
+        tc.tile_pool(name="results", bufs=2 * PAIR) as results,
+        tc.psum_pool(name="psum", bufs=2 * PAIR * OUT_BLOCKS) as psum,
+    ):
+        offsets = held.tile([P, N // 16], U16, name="offsets")
+        nc.sync.dma_start(offsets[:], offs)
+        windows = [held.tile([P, S], F32, name=f"window{r}") for r in range(ROW_BLOCKS)]
+        nc.sync.dma_start(windows[0][:], tab[0:P, :])
+        weights = held.tile([P, ROW_BLOCKS, M], BF16, name="weights")
+        nc.sync.dma_start(weights[:], w.rearrange("(r p) m -> p r m", p=P))
+        nc.sync.dma_start(windows[1][:], tab[P : 2 * P, :])
+        bias = held.tile([P, OUT_BLOCKS], F32, name="bias")
+        with nc.allow_non_contiguous_dma(reason="256 bias values, one to a partition and column"):
+            nc.sync.dma_start(bias[:], b.rearrange("(m p) o -> p (m o)", p=P))
+
+        for first in range(0, PIECES, PAIR):
+            pair = range(first, first + PAIR)
+            sums = {
+                (piece, m): psum.tile([P, PIECE], F32, name="sums")
+                for piece in pair
+                for m in range(OUT_BLOCKS)
+            }
+            for r in range(ROW_BLOCKS):
+                for piece in pair:
+                    entries = offsets[:, piece * PIECE_COLS : (piece + 1) * PIECE_COLS]
+                    x = looked_up.tile([P, PIECE], BF16, name="x")
+                    nc.vector.tensor_scalar(x[:], windows[r][:].indirect(entries), SCALE, -SHIFT * SCALE, MULT, ADD)
+                    for m in range(OUT_BLOCKS):
+                        nc.tensor.matmul(
+                            sums[piece, m][:],
+                            weights[:, r, m * P : (m + 1) * P],
+                            x[:],
+                            start=(r == 0),
+                            stop=(r == ROW_BLOCKS - 1),
+                        )
+            for piece in pair:
+                for m in range(OUT_BLOCKS):
+                    result = results.tile([P, PIECE], F32, name="result")
+                    if piece == PIECES - 1 and m == OUT_BLOCKS - 1:
+                        nc.vector.tensor_scalar_add(result[:], sums[piece, m][:], bias[:, m : m + 1])
+                    else:
+                        nc.scalar.activation(result[:], sums[piece, m][:], IDENTITY, bias=bias[:, m : m + 1])
+                    nc.sync.dma_start(
+                        out[m * P : (m + 1) * P, piece * PIECE : (piece + 1) * PIECE], result[:]
+                    )

@@ -11,7 +11,7 @@ OUT_BLOCKS = M // P
 PIECE = 512
 PIECES = N // PIECE
 PIECE_COLS = PIECE // 16
-PAIR = 2
+GROUPS = [(0, 1)] + [(piece,) for piece in range(2, PIECES)]
 
 SHIFT, SCALE = 0.125, 1.5
 
@@ -22,9 +22,9 @@ def tile_lookup_deq_nrm_bias_kernel(tc, tab, w, b, offs, out):
     nc = tc.nc
     with (
         tc.tile_pool(name="held", bufs=1) as held,
-        tc.tile_pool(name="looked_up", bufs=2 * PAIR) as looked_up,
-        tc.tile_pool(name="results", bufs=2 * PAIR) as results,
-        tc.psum_pool(name="psum", bufs=2 * PAIR * OUT_BLOCKS) as psum,
+        tc.tile_pool(name="looked_up", bufs=4) as looked_up,
+        tc.tile_pool(name="results", bufs=4) as results,
+        tc.psum_pool(name="psum", bufs=PIECES * OUT_BLOCKS) as psum,
     ):
         offsets = held.tile([P, N // 16], U16, name="offsets")
         nc.sync.dma_start(offsets[:], offs)
@@ -37,15 +37,14 @@ def tile_lookup_deq_nrm_bias_kernel(tc, tab, w, b, offs, out):
         with nc.allow_non_contiguous_dma(reason="256 bias values, one to a partition and column"):
             nc.sync.dma_start(bias[:], b.rearrange("(m p) o -> p (m o)", p=P))
 
-        for first in range(0, PIECES, PAIR):
-            pair = range(first, first + PAIR)
+        for group in GROUPS:
             sums = {
                 (piece, m): psum.tile([P, PIECE], F32, name="sums")
-                for piece in pair
+                for piece in group
                 for m in range(OUT_BLOCKS)
             }
             for r in range(ROW_BLOCKS):
-                for piece in pair:
+                for piece in group:
                     entries = offsets[:, piece * PIECE_COLS : (piece + 1) * PIECE_COLS]
                     x = looked_up.tile([P, PIECE], BF16, name="x")
                     nc.vector.tensor_scalar(x[:], windows[r][:].indirect(entries), SCALE, -SHIFT * SCALE, MULT, ADD)
@@ -57,7 +56,7 @@ def tile_lookup_deq_nrm_bias_kernel(tc, tab, w, b, offs, out):
                             start=(r == 0),
                             stop=(r == ROW_BLOCKS - 1),
                         )
-            for piece in pair:
+            for piece in group:
                 for m in range(OUT_BLOCKS):
                     result = results.tile([P, PIECE], F32, name="result")
                     if piece == PIECES - 1 and m == OUT_BLOCKS - 1:

@@ -12,6 +12,8 @@ PIECE = 512
 PIECES = N // PIECE
 PIECE_COLS = PIECE // 16
 GROUPS = [(0, 1)] + [(piece,) for piece in range(2, PIECES)]
+WHOLE = [(0, PIECE)]
+HALVES = [(0, PIECE // 2), (PIECE // 2, PIECE)]
 
 SHIFT, SCALE = 0.125, 1.5
 
@@ -59,10 +61,14 @@ def tile_lookup_deq_nrm_bias_kernel(tc, tab, w, b, offs, out):
             for piece in group:
                 for m in range(OUT_BLOCKS):
                     result = results.tile([P, PIECE], F32, name="result")
-                    if piece == PIECES - 1 and m == OUT_BLOCKS - 1:
-                        nc.vector.tensor_scalar_add(result[:], sums[piece, m][:], bias[:, m : m + 1])
-                    else:
-                        nc.scalar.activation(result[:], sums[piece, m][:], IDENTITY, bias=bias[:, m : m + 1])
-                    nc.sync.dma_start(
-                        out[m * P : (m + 1) * P, piece * PIECE : (piece + 1) * PIECE], result[:]
-                    )
+                    column_runs = HALVES if piece == PIECES - 1 else WHOLE
+                    for low, high in column_runs:
+                        product = sums[piece, m][:, low:high]
+                        if piece == PIECES - 1 and m == OUT_BLOCKS - 1:
+                            nc.vector.tensor_scalar_add(result[:, low:high], product, bias[:, m : m + 1])
+                        else:
+                            nc.scalar.activation(result[:, low:high], product, IDENTITY, bias=bias[:, m : m + 1])
+                        nc.sync.dma_start(
+                            out[m * P : (m + 1) * P, piece * PIECE + low : piece * PIECE + high],
+                            result[:, low:high],
+                        )

import concourse.mybir as mybir

F32, BF16, U16 = mybir.dt.float32, mybir.dt.bfloat16, mybir.dt.uint16
ADD, MULT = mybir.AluOpType.add, mybir.AluOpType.mult
IDENTITY = mybir.ActivationFunctionType.Identity

P = 128
K, S, N, M = 256, 2048, 2048, 256
ROW_BLOCKS = K // P
OUT_BLOCKS = M // P
PIECE = 512
PIECES = N // PIECE
PIECE_COLS = PIECE // 16
GROUPS = [(0, 1)] + [(piece,) for piece in range(2, PIECES)]
WHOLE = [(0, PIECE)]
HALVES = [(0, PIECE // 2), (PIECE // 2, PIECE)]

SHIFT, SCALE = 0.125, 1.5

FLOPS = 2 * K * M * N + 2 * K * N + M * N


def tile_lookup_deq_nrm_bias_kernel(tc, tab, w, b, offs, out):
    nc = tc.nc
    with (
        tc.tile_pool(name="held", bufs=1) as held,
        tc.tile_pool(name="looked_up", bufs=4) as looked_up,
        tc.tile_pool(name="results", bufs=4) as results,
        tc.psum_pool(name="psum", bufs=PIECES * OUT_BLOCKS) as psum,
    ):
        offsets = held.tile([P, N // 16], U16, name="offsets")
        nc.sync.dma_start(offsets[:], offs)
        windows = [held.tile([P, S], F32, name=f"window{r}") for r in range(ROW_BLOCKS)]
        nc.sync.dma_start(windows[0][:], tab[0:P, :])
        weights = held.tile([P, ROW_BLOCKS, M], BF16, name="weights")
        nc.sync.dma_start(weights[:], w.rearrange("(r p) m -> p r m", p=P))
        nc.sync.dma_start(windows[1][:], tab[P : 2 * P, :])
        bias = held.tile([P, OUT_BLOCKS], F32, name="bias")
        with nc.allow_non_contiguous_dma(reason="256 bias values, one to a partition and column"):
            nc.sync.dma_start(bias[:], b.rearrange("(m p) o -> p (m o)", p=P))

        for group in GROUPS:
            sums = {
                (piece, m): psum.tile([P, PIECE], F32, name="sums")
                for piece in group
                for m in range(OUT_BLOCKS)
            }
            for r in range(ROW_BLOCKS):
                for piece in group:
                    entries = offsets[:, piece * PIECE_COLS : (piece + 1) * PIECE_COLS]
                    x = looked_up.tile([P, PIECE], BF16, name="x")
                    nc.vector.tensor_scalar(x[:], windows[r][:].indirect(entries), SCALE, -SHIFT * SCALE, MULT, ADD)
                    for m in range(OUT_BLOCKS):
                        nc.tensor.matmul(
                            sums[piece, m][:],
                            weights[:, r, m * P : (m + 1) * P],
                            x[:],
                            start=(r == 0),
                            stop=(r == ROW_BLOCKS - 1),
                        )
            for piece in group:
                for m in range(OUT_BLOCKS):
                    result = results.tile([P, PIECE], F32, name="result")
                    column_runs = HALVES if piece == PIECES - 1 else WHOLE
                    for low, high in column_runs:
                        product = sums[piece, m][:, low:high]
                        if piece == PIECES - 1 and m == OUT_BLOCKS - 1:
                            nc.vector.tensor_scalar_add(result[:, low:high], product, bias[:, m : m + 1])
                        else:
                            nc.scalar.activation(result[:, low:high], product, IDENTITY, bias=bias[:, m : m + 1])
                        nc.sync.dma_start(
                            out[m * P : (m + 1) * P, piece * PIECE + low : piece * PIECE + high],
                            result[:, low:high],
                        )
